import numpy as np, ml_dtypes
CORES = [118,246,374,502,126,254,382,510]
N = 8
MB, TK = 12, 64
def setup_inputs(rng):
    return {"x": rng.standard_normal((N, MB, 128, TK), dtype=np.float32).astype(ml_dtypes.bfloat16), "w": (rng.standard_normal((N, 128, 128), dtype=np.float32) / 8).astype(ml_dtypes.bfloat16)}
def reference(x, w):
    def run(a, W, order):
        for s in order:
            a = np.maximum(np.einsum("kf,bkn->bfn", W[s].astype(np.float64), a), 0.0)
        return a
    dt = ml_dtypes.bfloat16 if x.dtype != np.float64 else np.float64
    y = np.full(x.shape, np.nan, dt)
    y[N - 1] = run(x[0].astype(np.float64), w, range(N)).astype(dt)
    return {"y": y}

@@ -1,0 +1,179 @@
+from concourse.mybir import dt, AluOpType
+
+N, MB, TK, P = 8, 12, 64, 128
+BANKS = 8
+XG = 4
+SEND = [[1, 1, 1], [1, 1, 1], [1, 1, 1], [1, 1, 1]]
+
+CHAINS, CHUNKS = [], []
+for _ws in SEND:
+    CHUNKS.append([])
+    for _k in _ws:
+        _m0 = CHAINS[-1][0] + CHAINS[-1][1] if CHAINS else 0
+        CHUNKS[-1].append(len(CHAINS))
+        CHAINS.append((_m0, _k))
+WIDEST = max(k for _, k in CHAINS) * TK
+
+SCRATCH = {
+    "wts": ("sbuf", [P, N * P], "bfloat16"),
+    "wq": ("sbuf", [P, XG * P], "bfloat16"),
+    "land": ("sbuf", [P, MB * TK], "bfloat16"),
+    "ha": ("sbuf", [P, MB * TK], "bfloat16"),
+    "hb": ("sbuf", [P, MB * TK], "bfloat16"),
+    "zero": ("sbuf", [P, WIDEST], "float32"),
+}
+for _b in range(BANKS):
+    SCRATCH["ps%d" % _b] = ("psum", [P, 512], "float32")
+
+SEMAPHORES = (["wl", "sent", "stored", "zs"] + ["wa%d" % l for l in range(N)] + ["arr%d" % c for c in range(len(CHUNKS))]
+              + ["xl%d" % c for c in range(MB // XG)]
+              + ["mm%d" % i for i in range(len(CHAINS))] + ["rl%d" % i for i in range(len(CHAINS))])
+
+
+def _engines(topo, src, dst):
+    return bin(topo.mask(src, dst)).count("1")
+
+
+def _links(topo, a, b):
+    if topo.host(a) == topo.host(b) and topo.chip(a) == topo.chip(b):
+        return 0
+    if topo.rack(topo.host(a)) == topo.rack(topo.host(b)):
+        return 1 if topo.mates(a, b) or topo.same_plane(a, b) else 2
+    return 1 if topo.chip(a) == topo.chip(b) else 3
+
+
+def _plan(cores, topo):
+    first, last = cores[0], cores[-1]
+    split = 0
+    while split < N - 1 and (cores[split] == first or topo.may_write(cores[split], first)):
+        split += 1
+    route = []
+    for l in range(N):
+        src, dst = cores[l], (first if l < split else last)
+        if src == dst:
+            route.append([src])
+        elif topo.may_write(src, dst):
+            route.append([src, dst])
+        else:
+            via = [r for r in cores if r not in (src, dst, first) and topo.may_write(src, r) and topo.may_write(r, dst)]
+            via.sort(key=lambda r: (_links(topo, src, r) + _links(topo, r, dst),
+                                    topo.rack(topo.host(r)) != topo.rack(topo.host(dst))))
+            route.append([src, via[0], dst])
+    return split, route
+
+
+def rank_program(g, core, T, topo):
+    rank = T.rank_of(core)
+    if rank is None:
+        return
+    cores, sem = T.cores, T.sem
+    first, last = cores[0], cores[-1]
+    split, route = _plan(cores, topo)
+    sent = [0]
+    queues = [g.sync, g.scalar]
+    KB = P // XG
+
+    def wslot(l):
+        return T.wts[:, l * P:(l + 1) * P]
+
+    def cols(m0, k):
+        return slice(m0 * TK, (m0 + k) * TK)
+
+    def push(dst, out_ap, in_ap, rsem):
+        rid, pid = topo.addr(dst, core)
+        g.remote_dma(out_ap, in_ap, remote_sem=rsem, local_sem=sem.sent, pid=pid, routing_id=rid,
+                     dma_engine_mask=topo.mask(core, dst))
+        sent[0] += _engines(topo, core, dst)
+
+    if core == first:
+        nq = 0
+        for a in range(XG):
+            queues[a % 2].dma_start(T.wq[a * KB:(a + 1) * KB, :], T.w[:, :]).then_inc(sem.wl, 16)
+            if a == 0:
+                queues[1].dma_start(T.land[:, cols(0, XG)], T.x[0:XG]).then_inc(sem.xl0, 16)
+        own_w = 16 * XG
+        for c in range(1, MB // XG):
+            queues[c % 2].dma_start(T.land[:, cols(c * XG, XG)], T.x[c * XG:(c + 1) * XG]).then_inc(sem["xl%d" % c], 16)
+    else:
+        g.scalar.dma_start(wslot(rank), T.w[:, :]).then_inc(sem.wl, 16)
+        own_w = 16
+    hops = sorted((r.index(core), l) for l, r in enumerate(route) if core in r[:-1])
+    for j, l in hops:
+        if j == 0:
+            g.wait_ge(sem.wl, own_w)
+        else:
+            g.wait_ge(sem["wa%d" % l], _engines(topo, route[l][j - 1], core))
+        push(route[l][j + 1], wslot(l), wslot(l), sem["wa%d" % l])
+
+    if core in (first, last):
+        layers = list(range(split)) if core == first else list(range(split, N))
+        nl = len(layers)
+        g.vector.memset(T.zero[:, :], 0.0).then_inc(sem.zs, 1)
+        g.vector.wait_ge(sem.zs, 1)
+
+        steps = [(c, li, i) for c, chs in enumerate(CHUNKS) for li in range(nl) for i in chs]
+        if core == first:
+            steps.sort(key=lambda s: (s[0] + 1.5 * s[1], s[2]))
+        order = [(i, li) for _, li, i in steps]
+        chunk_of = {i: c for c, chs in enumerate(CHUNKS) for i in chs}
+
+        seen = {}
+
+        def pe_wait(name, val):
+            if seen.get(name, 0) < val:
+                g.tensor.wait_ge(sem[name], val)
+                seen[name] = val
+
+        bufs = [T.ha, T.hb]
+        done = [0] * len(CHAINS)
+        for t, (i, li) in enumerate(order):
+            l, (m0, k) = layers[li], CHAINS[i]
+            cs, n = cols(m0, k), k * TK
+            bank = T["ps%d" % (t % BANKS)]
+            if li > 0:
+                pe_wait("rl%d" % i, li)
+            elif core == first:
+                for c in range(m0 // XG, (m0 + k - 1) // XG + 1):
+                    pe_wait("xl%d" % c, 16)
+            else:
+                pe_wait("arr%d" % chunk_of[i], _engines(topo, first, core))
+            if len(route[l]) == 1:
+                pe_wait("wl", own_w)
+            else:
+                pe_wait("wa%d" % l, _engines(topo, route[l][-2], core))
+            if t >= BANKS:
+                pe_wait("rl%d" % order[t - BANKS][0], order[t - BANKS][1] + 1)
+            if core == first and li == 0:
+                for m in range(m0, m0 + k):
+                    rows = slice((m % XG) * KB, (m % XG + 1) * KB)
+                    for j in range(XG):
+                        at = (m // XG) * XG * TK + j * TK
+                        g.tensor.matmul(bank[:, (m - m0) * TK:(m - m0 + 1) * TK], T.wq[rows, j * P:(j + 1) * P],
+                                        T.land[rows, at:at + TK], start=(j == 0), stop=(j == XG - 1)
+                                        ).then_inc(sem["mm%d" % i], 1)
+                        done[i] += 1
+            else:
+                src = T.land if li == 0 else bufs[(li - 1) % 2]
+                g.tensor.matmul(bank[:, 0:n], wslot(l), src[:, cs], start=True, stop=True).then_inc(sem["mm%d" % i], 1)
+                done[i] += 1
+            g.vector.wait_ge(sem["mm%d" % i], done[i])
+            g.vector.tensor_tensor(bufs[li % 2][:, cs], bank[:, 0:n], T.zero[:, 0:n], op=AluOpType.max).then_inc(
+                sem["rl%d" % i], 1)
+        out = bufs[(nl - 1) % 2]
+
+        if core == first:
+            for c, chs in enumerate(CHUNKS):
+                for i in chs:
+                    g.wait_ge(sem["rl%d" % i], nl)
+                cs = cols(CHAINS[chs[0]][0], sum(CHAINS[i][1] for i in chs))
+                push(last, T.land[:, cs], out[:, cs], sem["arr%d" % c])
+        else:
+            for i, (m0, k) in enumerate(CHAINS):
+                for m in range(m0, m0 + k):
+                    q = queues[m % 2]
+                    q.wait_ge(sem["rl%d" % i], nl)
+                    q.dma_start(T.y[m], out[:, cols(m, 1)]).then_inc(sem.stored, 16)
+            g.sync.wait_ge(sem.stored, 16 * MB)
+
+    if sent[0]:
+        g.wait_ge(sem.sent, sent[0])

@@ -12,7 +12,10 @@ for _ws in SEND:
         _m0 = CHAINS[-1][0] + CHAINS[-1][1] if CHAINS else 0
         CHUNKS[-1].append(len(CHAINS))
         CHAINS.append((_m0, _k))
-WIDEST = max(k for _, k in CHAINS) * TK
+YS = [2, 2, 2, 2, 2, 2]
+YLAG = 0
+YGROUPS = [(sum(YS[:q]), s) for q, s in enumerate(YS)]
+WIDEST = max([k for _, k in CHAINS] + YS) * TK
 
 SCRATCH = {
     "wts": ("sbuf", [P, N * P], "bfloat16"),
@@ -27,6 +30,7 @@ for _b in range(BANKS):
 
 SEMAPHORES = (["wl", "sent", "stored", "zs"] + ["wa%d" % l for l in range(N)] + ["arr%d" % c for c in range(len(CHUNKS))]
               + ["xl%d" % c for c in range(MB // XG)]
+              + ["ym%d" % q for q in range(len(YS))] + ["yr%d" % q for q in range(len(YS))]
               + ["mm%d" % i for i in range(len(CHAINS))] + ["rl%d" % i for i in range(len(CHAINS))])
 
 
@@ -86,7 +90,6 @@ def rank_program(g, core, T, topo):
         sent[0] += _engines(topo, core, dst)
 
     if core == first:
-        nq = 0
         for a in range(XG):
             queues[a % 2].dma_start(T.wq[a * KB:(a + 1) * KB, :], T.w[:, :]).then_inc(sem.wl, 16)
             if a == 0:
@@ -111,11 +114,21 @@ def rank_program(g, core, T, topo):
         g.vector.memset(T.zero[:, :], 0.0).then_inc(sem.zs, 1)
         g.vector.wait_ge(sem.zs, 1)
 
-        steps = [(c, li, i) for c, chs in enumerate(CHUNKS) for li in range(nl) for i in chs]
-        if core == first:
-            steps.sort(key=lambda s: (s[0] + 1.5 * s[1], s[2]))
-        order = [(i, li) for _, li, i in steps]
         chunk_of = {i: c for c, chs in enumerate(CHUNKS) for i in chs}
+        if core == first:
+            steps = [(c, li, i) for c, chs in enumerate(CHUNKS) for li in range(nl) for i in chs]
+            steps.sort(key=lambda s: (s[0] + 1.5 * s[1], s[2]))
+            order = [(i, li) for _, li, i in steps]
+        else:
+            order, late = [], []
+            for c, chs in enumerate(CHUNKS):
+                for li in range(nl - 1):
+                    order += [(i, li) for i in chs]
+                    if late and li >= YLAG:
+                        order.append(late.pop(0))
+                top = CHAINS[chs[-1]][0] + CHAINS[chs[-1]][1]
+                late += [(None, q) for q, (m0, s) in enumerate(YGROUPS) if CHAINS[chs[0]][0] < m0 + s <= top]
+            order += late
 
         seen = {}
 
@@ -124,12 +137,39 @@ def rank_program(g, core, T, topo):
                 g.tensor.wait_ge(sem[name], val)
                 seen[name] = val
 
+        def w_ready(l):
+            if len(route[l]) == 1:
+                pe_wait("wl", own_w)
+            else:
+                pe_wait("wa%d" % l, _engines(topo, route[l][-2], core))
+
         bufs = [T.ha, T.hb]
+        out = bufs[(nl - 1) % 2]
         done = [0] * len(CHAINS)
+        read = []
         for t, (i, li) in enumerate(order):
+            bank = T["ps%d" % (t % BANKS)]
+            if i is None:
+                m0, s = YGROUPS[li]
+                l, kb = layers[-1], P // s
+                for i2, (c0, k2) in enumerate(CHAINS):
+                    if c0 < m0 + s and m0 < c0 + k2:
+                        pe_wait("rl%d" % i2, nl - 1)
+                w_ready(l)
+                if t >= BANKS:
+                    pe_wait(*read[t - BANKS])
+                for a in range(s):
+                    for j in range(s):
+                        g.tensor.matmul(bank[a * kb:(a + 1) * kb, j * TK:(j + 1) * TK], T.wts[:, l * P + j:(l + 1) * P:s],
+                                        bufs[(nl - 2) % 2][:, cols(m0 + a, 1)], start=True, stop=True
+                                        ).then_inc(sem["ym%d" % li], 1)
+                g.vector.wait_ge(sem["ym%d" % li], s * s)
+                g.vector.tensor_tensor(out[:, cols(m0, s)], bank[:, 0:s * TK], T.zero[:, 0:s * TK], op=AluOpType.max
+                                       ).then_inc(sem["yr%d" % li], 1)
+                read.append(("yr%d" % li, 1))
+                continue
             l, (m0, k) = layers[li], CHAINS[i]
             cs, n = cols(m0, k), k * TK
-            bank = T["ps%d" % (t % BANKS)]
             if li > 0:
                 pe_wait("rl%d" % i, li)
             elif core == first:
@@ -137,12 +177,9 @@ def rank_program(g, core, T, topo):
                     pe_wait("xl%d" % c, 16)
             else:
                 pe_wait("arr%d" % chunk_of[i], _engines(topo, first, core))
-            if len(route[l]) == 1:
-                pe_wait("wl", own_w)
-            else:
-                pe_wait("wa%d" % l, _engines(topo, route[l][-2], core))
+            w_ready(l)
             if t >= BANKS:
-                pe_wait("rl%d" % order[t - BANKS][0], order[t - BANKS][1] + 1)
+                pe_wait(*read[t - BANKS])
             if core == first and li == 0:
                 for m in range(m0, m0 + k):
                     rows = slice((m % XG) * KB, (m % XG + 1) * KB)
@@ -159,7 +196,7 @@ def rank_program(g, core, T, topo):
             g.vector.wait_ge(sem["mm%d" % i], done[i])
             g.vector.tensor_tensor(bufs[li % 2][:, cs], bank[:, 0:n], T.zero[:, 0:n], op=AluOpType.max).then_inc(
                 sem["rl%d" % i], 1)
-        out = bufs[(nl - 1) % 2]
+            read.append(("rl%d" % i, li + 1))
 
         if core == first:
             for c, chs in enumerate(CHUNKS):
@@ -168,12 +205,10 @@ def rank_program(g, core, T, topo):
                 cs = cols(CHAINS[chs[0]][0], sum(CHAINS[i][1] for i in chs))
                 push(last, T.land[:, cs], out[:, cs], sem["arr%d" % c])
         else:
-            for i, (m0, k) in enumerate(CHAINS):
-                for m in range(m0, m0 + k):
-                    q = queues[m % 2]
-                    q.wait_ge(sem["rl%d" % i], nl)
-                    q.dma_start(T.y[m], out[:, cols(m, 1)]).then_inc(sem.stored, 16)
-            g.sync.wait_ge(sem.stored, 16 * MB)
+            for q, (m0, s) in enumerate(YGROUPS):
+                queues[q % 2].wait_ge(sem["yr%d" % q], 1)
+                queues[q % 2].dma_start(T.y[m0:m0 + s], out[:, cols(m0, s)]).then_inc(sem.stored, 16)
+            g.sync.wait_ge(sem.stored, 16 * len(YGROUPS))
 
     if sent[0]:
         g.wait_ge(sem.sent, sent[0])

from concourse.mybir import dt, AluOpType

N, MB, TK, P = 8, 12, 64, 128
BANKS = 8
XG = 4
SEND = [[1, 1, 1], [1, 1, 1], [1, 1, 1], [1, 1, 1]]

CHAINS, CHUNKS = [], []
for _ws in SEND:
    CHUNKS.append([])
    for _k in _ws:
        _m0 = CHAINS[-1][0] + CHAINS[-1][1] if CHAINS else 0
        CHUNKS[-1].append(len(CHAINS))
        CHAINS.append((_m0, _k))
YS = [2, 2, 2, 2, 2, 2]
YLAG = 0
YGROUPS = [(sum(YS[:q]), s) for q, s in enumerate(YS)]
WIDEST = max([k for _, k in CHAINS] + YS) * TK

SCRATCH = {
    "wts": ("sbuf", [P, N * P], "bfloat16"),
    "wq": ("sbuf", [P, XG * P], "bfloat16"),
    "land": ("sbuf", [P, MB * TK], "bfloat16"),
    "ha": ("sbuf", [P, MB * TK], "bfloat16"),
    "hb": ("sbuf", [P, MB * TK], "bfloat16"),
    "zero": ("sbuf", [P, WIDEST], "float32"),
}
for _b in range(BANKS):
    SCRATCH["ps%d" % _b] = ("psum", [P, 512], "float32")

SEMAPHORES = (["wl", "sent", "stored", "zs"] + ["wa%d" % l for l in range(N)] + ["arr%d" % c for c in range(len(CHUNKS))]
              + ["xl%d" % c for c in range(MB // XG)]
              + ["ym%d" % q for q in range(len(YS))] + ["yr%d" % q for q in range(len(YS))]
              + ["mm%d" % i for i in range(len(CHAINS))] + ["rl%d" % i for i in range(len(CHAINS))])


def _engines(topo, src, dst):
    return bin(topo.mask(src, dst)).count("1")


def _links(topo, a, b):
    if topo.host(a) == topo.host(b) and topo.chip(a) == topo.chip(b):
        return 0
    if topo.rack(topo.host(a)) == topo.rack(topo.host(b)):
        return 1 if topo.mates(a, b) or topo.same_plane(a, b) else 2
    return 1 if topo.chip(a) == topo.chip(b) else 3


def _plan(cores, topo):
    first, last = cores[0], cores[-1]
    split = 0
    while split < N - 1 and (cores[split] == first or topo.may_write(cores[split], first)):
        split += 1
    route = []
    for l in range(N):
        src, dst = cores[l], (first if l < split else last)
        if src == dst:
            route.append([src])
        elif topo.may_write(src, dst):
            route.append([src, dst])
        else:
            via = [r for r in cores if r not in (src, dst, first) and topo.may_write(src, r) and topo.may_write(r, dst)]
            via.sort(key=lambda r: (_links(topo, src, r) + _links(topo, r, dst),
                                    topo.rack(topo.host(r)) != topo.rack(topo.host(dst))))
            route.append([src, via[0], dst])
    return split, route


def rank_program(g, core, T, topo):
    rank = T.rank_of(core)
    if rank is None:
        return
    cores, sem = T.cores, T.sem
    first, last = cores[0], cores[-1]
    split, route = _plan(cores, topo)
    sent = [0]
    queues = [g.sync, g.scalar]
    KB = P // XG

    def wslot(l):
        return T.wts[:, l * P:(l + 1) * P]

    def cols(m0, k):
        return slice(m0 * TK, (m0 + k) * TK)

    def push(dst, out_ap, in_ap, rsem):
        rid, pid = topo.addr(dst, core)
        g.remote_dma(out_ap, in_ap, remote_sem=rsem, local_sem=sem.sent, pid=pid, routing_id=rid,
                     dma_engine_mask=topo.mask(core, dst))
        sent[0] += _engines(topo, core, dst)

    if core == first:
        for a in range(XG):
            queues[a % 2].dma_start(T.wq[a * KB:(a + 1) * KB, :], T.w[:, :]).then_inc(sem.wl, 16)
            if a == 0:
                queues[1].dma_start(T.land[:, cols(0, XG)], T.x[0:XG]).then_inc(sem.xl0, 16)
        own_w = 16 * XG
        for c in range(1, MB // XG):
            queues[c % 2].dma_start(T.land[:, cols(c * XG, XG)], T.x[c * XG:(c + 1) * XG]).then_inc(sem["xl%d" % c], 16)
    else:
        g.scalar.dma_start(wslot(rank), T.w[:, :]).then_inc(sem.wl, 16)
        own_w = 16
    hops = sorted((r.index(core), l) for l, r in enumerate(route) if core in r[:-1])
    for j, l in hops:
        if j == 0:
            g.wait_ge(sem.wl, own_w)
        else:
            g.wait_ge(sem["wa%d" % l], _engines(topo, route[l][j - 1], core))
        push(route[l][j + 1], wslot(l), wslot(l), sem["wa%d" % l])

    if core in (first, last):
        layers = list(range(split)) if core == first else list(range(split, N))
        nl = len(layers)
        g.vector.memset(T.zero[:, :], 0.0).then_inc(sem.zs, 1)
        g.vector.wait_ge(sem.zs, 1)

        chunk_of = {i: c for c, chs in enumerate(CHUNKS) for i in chs}
        if core == first:
            steps = [(c, li, i) for c, chs in enumerate(CHUNKS) for li in range(nl) for i in chs]
            steps.sort(key=lambda s: (s[0] + 1.5 * s[1], s[2]))
            order = [(i, li) for _, li, i in steps]
        else:
            order, late = [], []
            for c, chs in enumerate(CHUNKS):
                for li in range(nl - 1):
                    order += [(i, li) for i in chs]
                    if late and li >= YLAG:
                        order.append(late.pop(0))
                top = CHAINS[chs[-1]][0] + CHAINS[chs[-1]][1]
                late += [(None, q) for q, (m0, s) in enumerate(YGROUPS) if CHAINS[chs[0]][0] < m0 + s <= top]
            order += late

        seen = {}

        def pe_wait(name, val):
            if seen.get(name, 0) < val:
                g.tensor.wait_ge(sem[name], val)
                seen[name] = val

        def w_ready(l):
            if len(route[l]) == 1:
                pe_wait("wl", own_w)
            else:
                pe_wait("wa%d" % l, _engines(topo, route[l][-2], core))

        bufs = [T.ha, T.hb]
        out = bufs[(nl - 1) % 2]
        done = [0] * len(CHAINS)
        read = []
        for t, (i, li) in enumerate(order):
            bank = T["ps%d" % (t % BANKS)]
            if i is None:
                m0, s = YGROUPS[li]
                l, kb = layers[-1], P // s
                for i2, (c0, k2) in enumerate(CHAINS):
                    if c0 < m0 + s and m0 < c0 + k2:
                        pe_wait("rl%d" % i2, nl - 1)
                w_ready(l)
                if t >= BANKS:
                    pe_wait(*read[t - BANKS])
                for a in range(s):
                    for j in range(s):
                        g.tensor.matmul(bank[a * kb:(a + 1) * kb, j * TK:(j + 1) * TK], T.wts[:, l * P + j:(l + 1) * P:s],
                                        bufs[(nl - 2) % 2][:, cols(m0 + a, 1)], start=True, stop=True
                                        ).then_inc(sem["ym%d" % li], 1)
                g.vector.wait_ge(sem["ym%d" % li], s * s)
                g.vector.tensor_tensor(out[:, cols(m0, s)], bank[:, 0:s * TK], T.zero[:, 0:s * TK], op=AluOpType.max
                                       ).then_inc(sem["yr%d" % li], 1)
                read.append(("yr%d" % li, 1))
                continue
            l, (m0, k) = layers[li], CHAINS[i]
            cs, n = cols(m0, k), k * TK
            if li > 0:
                pe_wait("rl%d" % i, li)
            elif core == first:
                for c in range(m0 // XG, (m0 + k - 1) // XG + 1):
                    pe_wait("xl%d" % c, 16)
            else:
                pe_wait("arr%d" % chunk_of[i], _engines(topo, first, core))
            w_ready(l)
            if t >= BANKS:
                pe_wait(*read[t - BANKS])
            if core == first and li == 0:
                for m in range(m0, m0 + k):
                    rows = slice((m % XG) * KB, (m % XG + 1) * KB)
                    for j in range(XG):
                        at = (m // XG) * XG * TK + j * TK
                        g.tensor.matmul(bank[:, (m - m0) * TK:(m - m0 + 1) * TK], T.wq[rows, j * P:(j + 1) * P],
                                        T.land[rows, at:at + TK], start=(j == 0), stop=(j == XG - 1)
                                        ).then_inc(sem["mm%d" % i], 1)
                        done[i] += 1
            else:
                src = T.land if li == 0 else bufs[(li - 1) % 2]
                g.tensor.matmul(bank[:, 0:n], wslot(l), src[:, cs], start=True, stop=True).then_inc(sem["mm%d" % i], 1)
                done[i] += 1
            g.vector.wait_ge(sem["mm%d" % i], done[i])
            g.vector.tensor_tensor(bufs[li % 2][:, cs], bank[:, 0:n], T.zero[:, 0:n], op=AluOpType.max).then_inc(
                sem["rl%d" % i], 1)
            read.append(("rl%d" % i, li + 1))

        if core == first:
            for c, chs in enumerate(CHUNKS):
                for i in chs:
                    g.wait_ge(sem["rl%d" % i], nl)
                cs = cols(CHAINS[chs[0]][0], sum(CHAINS[i][1] for i in chs))
                push(last, T.land[:, cs], out[:, cs], sem["arr%d" % c])
        else:
            for q, (m0, s) in enumerate(YGROUPS):
                queues[q % 2].wait_ge(sem["yr%d" % q], 1)
                queues[q % 2].dma_start(T.y[m0:m0 + s], out[:, cols(m0, s)]).then_inc(sem.stored, 16)
            g.sync.wait_ge(sem.stored, 16 * len(YGROUPS))

    if sent[0]:
        g.wait_ge(sem.sent, sent[0])
